import numpy as np
import ml_dtypes


def mxq(x, axis, fmt="e4m3"):
    dtype, down = {"e4m3": (ml_dtypes.float8_e4m3fn, 7), "e5m2": (ml_dtypes.float8_e5m2, 14)}[fmt]
    v = np.moveaxis(np.asarray(x, np.float32).astype(ml_dtypes.bfloat16).astype(np.float64), axis, -1)
    blocks = v.reshape(v.shape[:-1] + (-1, 32))
    amax = np.abs(blocks).max(-1, keepdims=True)
    byte = np.maximum(np.where(amax > 0, np.frexp(amax)[1] - 1 + 127, 0) - down, 1)
    scale = np.exp2(byte - 127.0)
    codes = (blocks / scale).astype(np.float32).astype(dtype).astype(np.float64)
    return np.moveaxis((codes * scale).reshape(v.shape), -1, axis)


WIDE = False


def mx_kscale(k):
    if not WIDE:
        return np.ones(k)
    levels = np.array([18, -18])
    if k % 512:
        return np.exp2(np.random.permutation(np.resize(levels, k // 32))).repeat(32)
    a = np.empty((k // 512, 16))
    for p in range(k // 512):
        a[p, :8] = np.random.permutation(np.resize(levels, 8))
        for g in range(8):
            far = levels[np.abs(levels - a[p, g]) >= 10]
            a[p, g + 8] = far[np.random.randint(len(far))]
    return np.exp2(a.ravel()).repeat(32)


def f64(x):
    return np.asarray(x).astype(np.float64)


def striped(idx):
    return np.tile(np.asarray(idx).reshape(-1, 16).T, (8, 1)).astype(np.uint16)


def unstriped(offs):
    return offs[:16].T.reshape(-1).astype(np.int64)


def sig(x):
    return 1.0 / (1.0 + np.exp(-x))


def setup_inputs():
    n = np.random.standard_normal
    uni = np.random.uniform
    idx = np.random.permutation(2048)[:512]
    f_d = mx_kscale(512)
    f_e = mx_kscale(512)
    f_i = np.ones(2048)
    f_i[idx] = mx_kscale(512)
    return {
        "qT": (n((512, 512)) * f_d[:, None]).astype(np.float32),
        "kT": (n((512, 2048)) / np.sqrt(512) / f_d[:, None] * f_i[None, :]).astype(np.float32),
        "vT": (n((512, 2048)) / np.sqrt(512) * f_e[:, None] * f_i[None, :]).astype(np.float32),
        "dy": (np.round(n((512, 512)) * 8) / 8).astype(np.float32),
        "u": (np.round(n((512, 512)) * 8) / 8 / f_e[None, :]).astype(np.float32),
        "us": (uni(0.75, 1.3, (512, 1))).astype(np.float32),
        "ts": np.tile(uni(0.75, 1.3, 2048) / f_i, (128, 1)).astype(np.float32),
        "tv": np.tile(uni(0.75, 1.3, 2048) / f_i, (128, 1)).astype(np.float32),
        "offs": striped(idx),
    }


def reference(qT, kT, vT, dy, u, us, ts, tv, offs):
    idx = unstriped(offs)
    kT_i = f64(kT)[:, idx]
    vT_i = f64(vT)[:, idx]
    ts_i = f64(ts)[:1][:, idx]
    tv_i = f64(tv)[:1][:, idx]
    a = mxq(f64(qT), 0, "e4m3").T @ mxq(kT_i, 0, "e4m3")
    s = sig(f64(us) * ts_i * a)
    w = tv_i * s
    o = mxq(w, 1, "e4m3") @ mxq(vT_i, 1, "e4m3").T
    out_0 = f64(dy) * o
    do = f64(dy) * f64(u)
    b = mxq(do, 1, "e5m2") @ mxq(vT_i, 0, "e4m3")
    g = f64(us) * ts_i * tv_i * s * (1.0 - s) * b
    out_1 = mxq(g, 1, "e5m2") @ mxq(kT_i, 1, "e4m3").T
    return out_0, out_1

@@ -1,0 +1,241 @@
+from contextlib import ExitStack
+
+import concourse.mybir as mybir
+from concourse.masks import make_identity
+
+F32 = mybir.dt.float32
+BF16 = mybir.dt.bfloat16
+U32 = mybir.dt.uint32
+U16 = mybir.dt.uint16
+U8 = mybir.dt.uint8
+E4M3 = mybir.dt.float8_e4m3fn_x4
+E5M2 = mybir.dt.float8_e5m2_x4
+ACT = mybir.ActivationFunctionType
+ALU = mybir.AluOpType
+
+P = 128
+PACK = 4
+N = 512
+TOKENS = 2048
+BLOCKS = N // P
+LAST = P - 1
+
+FLOPS = 4 * 2 * N * N * N
+BYTES = 4 * (2 * N * TOKENS + 5 * N * N + N + 2 * TOKENS) + 2 * P * (N // 16)
+
+
+def tile_attend_ggau_kernel(tc, qT, kT, vT, dy, u, us, ts, tv, offs, out_0, out_1):
+    nc = tc.nc
+    with ExitStack() as ctx:
+        keep = ctx.enter_context(tc.tile_pool(name="keep", bufs=1))
+        ring = ctx.enter_context(tc.tile_pool(name="ring", bufs=4))
+        sums = ctx.enter_context(tc.psum_pool(name="sums", bufs=4))
+        turns = ctx.enter_context(tc.psum_pool(name="turns", bufs=4))
+
+        def sb(name, cols, dtype):
+            return keep.tile([P, cols], dtype, name=name, align_bytes=64)
+
+        def ring_tile(tag, dtype):
+            return ring.tile([P, N], dtype, name=tag, tag=tag, align_bytes=64)
+
+        offsets = keep.tile([P, N // 16], U16, name="offsets")
+        nc.sync.dma_start(offsets[:], offs)
+
+        ts_window = sb("ts_window", TOKENS, F32)
+        tv_window = sb("tv_window", TOKENS, F32)
+        us_row = sb("us_row", N, F32)
+        nc.sync.dma_start(ts_window[LAST:P, :], ts[0:1, :])
+        nc.sync.dma_start(tv_window[LAST:P, :], tv[0:1, :])
+        nc.sync.dma_start(us_row[LAST:P, :], us.rearrange("r o -> o r"))
+        k_planes = [sb("k_plane%d" % t, TOKENS, F32) for t in range(PACK)]
+        v_planes = [sb("v_plane%d" % t, TOKENS, F32) for t in range(PACK)]
+        q_halves = [keep.tile([P, PACK, N // 2], F32, name="q_half%d" % h) for h in range(2)]
+        dy_blocks = [sb("dy%d" % j, N, F32) for j in range(BLOCKS)]
+        u_blocks = [sb("u%d" % j, N, F32) for j in range(BLOCKS)]
+        kT_planes = kT.rearrange("(p t) w -> t p w", t=PACK)
+        vT_planes = vT.rearrange("(p t) w -> t p w", t=PACK)
+        qT_rows = qT.rearrange("(p t) r -> p t r", t=PACK)
+        for t in range(PACK):
+            nc.sync.dma_start(k_planes[t][:], kT_planes[t])
+        for h in range(2):
+            nc.sync.dma_start(q_halves[h][:], qT_rows[:, :, h * (N // 2):(h + 1) * (N // 2)])
+        for t in range(PACK):
+            nc.sync.dma_start(v_planes[t][:], vT_planes[t])
+        for j in range(BLOCKS):
+            nc.sync.dma_start(dy_blocks[j][:], dy[j * P:(j + 1) * P, :])
+            nc.sync.dma_start(u_blocks[j][:], u[j * P:(j + 1) * P, :])
+
+        zero = keep.tile([P, 1], F32, name="zero")
+        half = keep.tile([P, 1], F32, name="half")
+        nc.vector.memset(zero[:], 0.0)
+        nc.scalar.activation(half[:], zero[:], ACT.Sigmoid)
+
+        nc.vector.memset(ts_window[0:LAST, :], 0.0)
+        nc.vector.memset(tv_window[0:LAST, :], 0.0)
+        nc.vector.memset(us_row[0:LAST, :], 0.0)
+        identity = sb("identity", P, F32)
+        make_identity(nc, identity[:])
+
+        def gather(out, window):
+            nc.vector.tensor_copy(out, window[:].indirect(offsets[:]))
+
+        def quantise(name, values, fmt):
+            words = values.shape[1] // PACK
+            codes = sb(name + "_codes", words, U32)
+            scales = sb(name + "_scales", words, U8)
+            nc.vector.quantize_mx(out=codes[:].bitcast(fmt), scales=scales[:], in_=values)
+            return codes, scales
+
+        def quantise_into(codes, scales, cols, values, fmt):
+            nc.vector.quantize_mx(out=codes[:, cols].bitcast(fmt), scales=scales[:, cols], in_=values)
+
+        def row_to_columns(name, row):
+            bank = turns.tile([P, N], F32, name="bank", tag="turn")
+            for j in range(BLOCKS):
+                nc.tensor.transpose(bank[:, j * P:(j + 1) * P], row[:, j * P:(j + 1) * P], identity[:])
+            columns = keep.tile([P, BLOCKS], F32, name=name)
+            nc.scalar.copy(columns[:], bank[:, LAST:N:P])
+            return columns
+
+        def columns_to_rows(name, columns):
+            bank = turns.tile([P, N], F32, name="bank", tag="turn")
+            for j in range(BLOCKS):
+                nc.tensor.transpose(bank[:, j * P:(j + 1) * P], columns[:, j:j + 1].to_broadcast([P, P]), identity[:])
+            rows = sb(name, N, F32)
+            nc.scalar.copy(rows[:], bank[:])
+            return rows
+
+        def turn_words(bank, slot, values):
+            words = values.bitcast(F32)
+            for w in range(2):
+                at = (2 * slot + w) * P
+                nc.tensor.transpose(bank[:, at:at + P], words[:, w:N // 2:2], identity[:])
+
+        def interleave(engine_copy, out, planes):
+            engine_copy(out.rearrange("p (c i t) -> p c t i", i=4, t=PACK), planes.rearrange("p t (c i) -> p c t i", i=4))
+
+        def product(lhs, lhs_fmt, rhs):
+            bank = sums.tile([P, N], F32, name="sum", tag="sum")
+            nc.tensor.matmul_mx(out=bank[:], lhsT=lhs[0].bitcast(lhs_fmt), lhsT_scale=lhs[1],
+                                rhs=rhs[0][:].bitcast(E4M3), rhs_scale=rhs[1][:], start=True, stop=True)
+            return bank
+
+        def gather_and_turn(name, planes, picked, along_slots, h):
+            bank = turns.tile([P, N], F32, name="bank", tag="turn")
+            for t2 in range(2):
+                t = 2 * h + t2
+                gather(picked[:, t * N:(t + 1) * N], planes[t])
+                turn_words(bank, t2, picked[:, t * N:(t + 1) * N])
+            turned = along_slots[:, h * 2 * N:(h + 1) * 2 * N]
+            nc.scalar.copy(turned.bitcast(F32).rearrange("s (p x) -> s p x", x=4),
+                           bank[:].rearrange("s (x p) -> s p x", x=4))
+            return turned
+
+        def turn_block(name, values):
+            bank = turns.tile([P, N], F32, name="bank", tag="turn")
+            turn_words(bank, 0, values)
+            turned = sb(name + "_turned", N, BF16)
+            nc.scalar.copy(turned[:].bitcast(F32).rearrange("s (r w) -> s r w", w=2),
+                           bank[:, 0:2 * P].rearrange("s (w r) -> s r w", w=2))
+            return turned
+
+        def in_feature_order(bank):
+            return bank[:].rearrange("r (h p t) -> r p h t", h=2, t=2)
+
+        def as_features(tile):
+            return tile[:].rearrange("r (p h t) -> r p h t", h=2, t=2)
+
+        half_cols = [slice(h * (N // 2), (h + 1) * (N // 2)) for h in range(2)]
+
+        k_picked = sb("k_picked", PACK * N, BF16)
+        k_turned = sb("k_turned", PACK * N, BF16)
+        k_turned0 = gather_and_turn("k", k_planes, k_picked, k_turned, 0)
+        ts_picked = sb("ts_picked", N, F32)
+        tv_picked = sb("tv_picked", N, F32)
+        gather(ts_picked[:], ts_window)
+        gather(tv_picked[:], tv_window)
+        us_cols = row_to_columns("us_cols", us_row)
+        ts_cols = row_to_columns("ts_cols", ts_picked)
+        tv_cols = row_to_columns("tv_cols", tv_picked)
+        neg_c_cols = keep.tile([P, BLOCKS], F32, name="neg_c_cols")
+        nc.vector.scalar_tensor_tensor(neg_c_cols[:], ts_cols[:], -1.0, tv_cols[:], ALU.mult, ALU.mult)
+        ts_rows = columns_to_rows("ts_rows", ts_cols)
+        tv_rows = columns_to_rows("tv_rows", tv_cols)
+        neg_c_rows = columns_to_rows("neg_c_rows", neg_c_cols)
+        k_turned1 = gather_and_turn("k", k_planes, k_picked, k_turned, 1)
+        k_words = sb("k_words", PACK * N, BF16)
+        interleave(nc.vector.tensor_copy, k_words[:], k_picked[:].rearrange("p (t i) -> p t i", t=PACK))
+        k_features = quantise("k_features", k_words[:], E4M3)
+
+        q_mx = []
+        for h in range(2):
+            q_words = sb("q_words%d" % h, PACK * N // 2, BF16)
+            interleave(nc.scalar.copy, q_words[:], q_halves[h][:])
+            q_mx.append(quantise("q%d" % h, q_words[:], E4M3))
+
+        v_picked = sb("v_picked", PACK * N, BF16)
+        v_turned = sb("v_turned", PACK * N, BF16)
+
+        def scores(j):
+            codes, scales = q_mx[j // 2]
+            cols = slice((j % 2) * P, (j % 2 + 1) * P)
+            a = product((codes[:, cols], scales[:, cols]), E4M3, k_features)
+            z = sb("z%d" % j, N, F32)
+            nc.vector.tensor_tensor(z[:], a[:], ts_rows[:], ALU.mult)
+            s = sb("s%d" % j, N, F32)
+            nc.scalar.activation(s[:], z[:], ACT.Sigmoid, scale=us_cols[:, j:j + 1])
+            sq = sb("sq%d" % j, N, F32)
+            nc.scalar.activation(sq[:], s[:], ACT.Square, scale=-1.0, bias=half[:])
+            return s, sq
+
+        def weights(j, s, sq):
+            w = ring_tile("rounded", BF16)
+            nc.vector.tensor_tensor(w[:], s[:], tv_rows[:], ALU.mult)
+            w_turned = turn_block("w%d" % j, w[:])
+            m = sb("m%d" % j, N, F32)
+            nc.vector.scalar_tensor_tensor(m[:], sq[:], -0.25, neg_c_rows[:], ALU.add, ALU.mult)
+            return w_turned, m
+
+        def gate_gradient(j):
+            o = product((w_mx[j][0][:], w_mx[j][1][:]), E4M3, v_slots)
+            result = sb("result0_%d" % j, N, F32)
+            nc.vector.tensor_tensor(as_features(result), in_feature_order(o), as_features(dy_blocks[j]), ALU.mult)
+            nc.sync.dma_start(out_0[j * P:(j + 1) * P, :], result[:])
+
+        def output_gradient(j):
+            do = ring_tile("rounded", BF16)
+            nc.vector.tensor_tensor(do[:], dy_blocks[j][:], u_blocks[j][:], ALU.mult)
+            return turn_block("do%d" % j, do[:])
+
+        def score_gradient(j, do_mx):
+            b = product((do_mx[0][:], do_mx[1][:]), E5M2, v_features)
+            g = ring_tile("rounded", BF16)
+            nc.vector.scalar_tensor_tensor(g[:], b[:], us_cols[:, j:j + 1], wm[j][1][:], ALU.mult, ALU.mult)
+            return turn_block("g%d" % j, g[:])
+
+        def query_gradient(j, g_mx):
+            dq = product((g_mx[0][:], g_mx[1][:]), E5M2, k_slots)
+            result = sb("result1_%d" % j, N, F32)
+            nc.scalar.copy(as_features(result), in_feature_order(dq))
+            nc.sync.dma_start(out_1[j * P:(j + 1) * P, :], result[:])
+
+
+        ssq = [scores(j) for j in range(2)]
+        gather_and_turn("v", v_planes, v_picked, v_turned, 0)
+        ssq.extend([scores(j) for j in range(2, 4)])
+        gather_and_turn("v", v_planes, v_picked, v_turned, 1)
+        v_words = sb("v_words", PACK * N, BF16)
+        interleave(nc.scalar.copy, v_words[:], v_picked[:].rearrange("p (t i) -> p t i", t=PACK))
+        v_features = quantise("v_features", v_words[:], E4M3)
+        wm = [weights(j, ssq[j][0], ssq[j][1]) for j in range(BLOCKS)]
+        v_slots = quantise("v_slots", v_turned[:], E4M3)
+        g_turned = []
+        for j in range(BLOCKS):
+            do_mx = quantise("do%d" % j, output_gradient(j)[:], E5M2)
+            g_turned.append(score_gradient(j, do_mx))
+        k_slots = quantise("k_slots", k_turned[:], E4M3)
+        for j in range(BLOCKS):
+            query_gradient(j, quantise("g%d" % j, g_turned[j][:], E5M2))
+        w_mx = [quantise("w%d" % j, wm[j][0][:], E4M3) for j in range(BLOCKS)]
+        for j in range(BLOCKS):
+            gate_gradient(j)

@@ -16,9 +16,14 @@ ALU = mybir.AluOpType
 P = 128
 PACK = 4
 N = 512
+HALF = N // 2
 TOKENS = 2048
 BLOCKS = N // P
 LAST = P - 1
+
+VECTOR_TILES = 33
+SCALAR_TILES = 18
+PASSING_BANKS = 7
 
 FLOPS = 4 * 2 * N * N * N
 BYTES = 4 * (2 * N * TOKENS + 5 * N * N + N + 2 * TOKENS) + 2 * P * (N // 16)
@@ -28,116 +33,150 @@ def tile_attend_ggau_kernel(tc, qT, kT, vT, dy, u, us, ts, tv, offs, out_0, out_
     nc = tc.nc
     with ExitStack() as ctx:
         keep = ctx.enter_context(tc.tile_pool(name="keep", bufs=1))
-        ring = ctx.enter_context(tc.tile_pool(name="ring", bufs=4))
-        sums = ctx.enter_context(tc.psum_pool(name="sums", bufs=4))
-        turns = ctx.enter_context(tc.psum_pool(name="turns", bufs=4))
+        scalar_ring = ctx.enter_context(tc.tile_pool(name="scalar_ring", bufs=SCALAR_TILES))
+        vector_ring = ctx.enter_context(tc.tile_pool(name="vector_ring", bufs=VECTOR_TILES))
+        banks = ctx.enter_context(tc.psum_pool(name="banks", bufs=PASSING_BANKS))
+        held = ctx.enter_context(tc.psum_pool(name="held", bufs=1))
 
-        def sb(name, cols, dtype):
+        def kept(name, cols, dtype):
             return keep.tile([P, cols], dtype, name=name, align_bytes=64)
 
-        def ring_tile(tag, dtype):
-            return ring.tile([P, N], dtype, name=tag, tag=tag, align_bytes=64)
+        def by_scalar(name, cols, dtype):
+            return scalar_ring.tile([P, cols], dtype, name=name, tag="by_scalar", align_bytes=64)
+
+        def by_vector(name, cols, dtype):
+            return vector_ring.tile([P, cols], dtype, name=name, tag="by_vector", align_bytes=64)
+
+        def new_bank():
+            return banks.tile([P, N], F32, name="bank", tag="bank")
 
         offsets = keep.tile([P, N // 16], U16, name="offsets")
         nc.sync.dma_start(offsets[:], offs)
 
-        ts_window = sb("ts_window", TOKENS, F32)
-        tv_window = sb("tv_window", TOKENS, F32)
-        us_row = sb("us_row", N, F32)
+        ts_window = kept("ts_window", TOKENS, F32)
+        tv_window = kept("tv_window", TOKENS, F32)
+        us_row = kept("us_row", N, F32)
         nc.sync.dma_start(ts_window[LAST:P, :], ts[0:1, :])
         nc.sync.dma_start(tv_window[LAST:P, :], tv[0:1, :])
         nc.sync.dma_start(us_row[LAST:P, :], us.rearrange("r o -> o r"))
-        k_planes = [sb("k_plane%d" % t, TOKENS, F32) for t in range(PACK)]
-        v_planes = [sb("v_plane%d" % t, TOKENS, F32) for t in range(PACK)]
-        q_halves = [keep.tile([P, PACK, N // 2], F32, name="q_half%d" % h) for h in range(2)]
-        dy_blocks = [sb("dy%d" % j, N, F32) for j in range(BLOCKS)]
-        u_blocks = [sb("u%d" % j, N, F32) for j in range(BLOCKS)]
-        kT_planes = kT.rearrange("(p t) w -> t p w", t=PACK)
-        vT_planes = vT.rearrange("(p t) w -> t p w", t=PACK)
-        qT_rows = qT.rearrange("(p t) r -> p t r", t=PACK)
+
+        k_planes = [kept("k_plane%d" % t, TOKENS, F32) for t in range(PACK)]
+        v_planes = [kept("v_plane%d" % t, TOKENS, F32) for t in range(PACK)]
+        q_halves = [keep.tile([P, PACK, HALF], F32, name="q_half%d" % h) for h in range(2)]
+        dy_blocks = [kept("dy%d" % j, N, F32) for j in range(BLOCKS)]
+        u_blocks = [kept("u%d" % j, N, F32) for j in range(BLOCKS)]
         for t in range(PACK):
-            nc.sync.dma_start(k_planes[t][:], kT_planes[t])
+            nc.sync.dma_start(k_planes[t][:], kT.rearrange("(p t) w -> t p w", t=PACK)[t])
+
+        zero = keep.tile([P, 1], F32, name="zero")
+        one_half = keep.tile([P, 1], F32, name="one_half")
+        nc.vector.memset(zero[:], 0.0)
+        nc.scalar.activation(one_half[:], zero[:], ACT.Sigmoid)
+
+        identity = kept("identity", P, F32)
+        make_identity(nc, identity[:])
+        nc.vector.memset(ts_window[0:LAST, :], 0.0)
+        nc.gpsimd.memset(tv_window[0:LAST, :], 0.0)
+        nc.vector.memset(us_row[0:LAST, :], 0.0)
+
         for h in range(2):
-            nc.sync.dma_start(q_halves[h][:], qT_rows[:, :, h * (N // 2):(h + 1) * (N // 2)])
+            nc.sync.dma_start(q_halves[h][:], qT.rearrange("(p t) r -> p t r", t=PACK)[:, :, h * HALF:(h + 1) * HALF])
         for t in range(PACK):
-            nc.sync.dma_start(v_planes[t][:], vT_planes[t])
+            nc.sync.dma_start(v_planes[t][:], vT.rearrange("(p t) w -> t p w", t=PACK)[t])
         for j in range(BLOCKS):
             nc.sync.dma_start(dy_blocks[j][:], dy[j * P:(j + 1) * P, :])
             nc.sync.dma_start(u_blocks[j][:], u[j * P:(j + 1) * P, :])
-
-        zero = keep.tile([P, 1], F32, name="zero")
-        half = keep.tile([P, 1], F32, name="half")
-        nc.vector.memset(zero[:], 0.0)
-        nc.scalar.activation(half[:], zero[:], ACT.Sigmoid)
-
-        nc.vector.memset(ts_window[0:LAST, :], 0.0)
-        nc.vector.memset(tv_window[0:LAST, :], 0.0)
-        nc.vector.memset(us_row[0:LAST, :], 0.0)
-        identity = sb("identity", P, F32)
-        make_identity(nc, identity[:])
 
         def gather(out, window):
             nc.vector.tensor_copy(out, window[:].indirect(offsets[:]))
 
         def quantise(name, values, fmt):
             words = values.shape[1] // PACK
-            codes = sb(name + "_codes", words, U32)
-            scales = sb(name + "_scales", words, U8)
-            nc.vector.quantize_mx(out=codes[:].bitcast(fmt), scales=scales[:], in_=values)
+            codes = by_vector(name + "_codes", words, U32)
+            scales = kept(name + "_scales", words, U8)
+            nc.vector.quantize_mx(out=codes[:].bitcast(fmt), scales=scales[:], in_=values[:])
             return codes, scales
 
-        def quantise_into(codes, scales, cols, values, fmt):
-            nc.vector.quantize_mx(out=codes[:, cols].bitcast(fmt), scales=scales[:, cols], in_=values)
+        def quantise_halves(name, halves):
+            codes = by_vector(name + "_codes", N, U32)
+            scales = kept(name + "_scales", N, U8)
+            for h in (1, 0):
+                cols = slice(h * HALF, (h + 1) * HALF)
+                nc.vector.quantize_mx(out=codes[:, cols].bitcast(E4M3), scales=scales[:, cols], in_=halves[h][:])
+            return codes, scales
+
+        def block_of(operand, j):
+            cols = slice(j * P, (j + 1) * P)
+            return operand[0][:, cols], operand[1][:, cols]
+
+        def mx_pass(out, stationary, stationary_fmt, moving):
+            nc.tensor.matmul_mx(out=out, lhsT=stationary[0].bitcast(stationary_fmt), lhsT_scale=stationary[1],
+                                rhs=moving[0][:].bitcast(E4M3), rhs_scale=moving[1][:], start=True, stop=True)
+
+        def product(stationary, stationary_fmt, moving):
+            bank = new_bank()
+            mx_pass(bank[:], stationary, stationary_fmt, moving)
+            return bank
+
+        def dealt(row):
+            return row.rearrange("p (s w e) -> p w s e", w=2, e=2)
+
+        def as_dealt(row):
+            return row.rearrange("p (w s e) -> p w s e", w=2, e=2)
+
+        def gathered_scale(name, window):
+            picked = kept(name + "_picked", N, F32)
+            gather(picked[:], window)
+            row = by_scalar(name + "_dealt", N, F32)
+            nc.scalar.copy(as_dealt(row[:]), dealt(picked[:]))
+            return row
 
         def row_to_columns(name, row):
-            bank = turns.tile([P, N], F32, name="bank", tag="turn")
+            bank = new_bank()
             for j in range(BLOCKS):
                 nc.tensor.transpose(bank[:, j * P:(j + 1) * P], row[:, j * P:(j + 1) * P], identity[:])
             columns = keep.tile([P, BLOCKS], F32, name=name)
             nc.scalar.copy(columns[:], bank[:, LAST:N:P])
             return columns
 
-        def columns_to_rows(name, columns):
-            bank = turns.tile([P, N], F32, name="bank", tag="turn")
+        def columns_to_rows(bank, columns):
             for j in range(BLOCKS):
                 nc.tensor.transpose(bank[:, j * P:(j + 1) * P], columns[:, j:j + 1].to_broadcast([P, P]), identity[:])
-            rows = sb(name, N, F32)
-            nc.scalar.copy(rows[:], bank[:])
-            return rows
 
-        def turn_words(bank, slot, values):
-            words = values.bitcast(F32)
-            for w in range(2):
-                at = (2 * slot + w) * P
-                nc.tensor.transpose(bank[:, at:at + P], words[:, w:N // 2:2], identity[:])
+        def gather_plane(picked, planes, t):
+            gather(picked[:, t * N:(t + 1) * N], planes[t])
 
-        def interleave(engine_copy, out, planes):
-            engine_copy(out.rearrange("p (c i t) -> p c t i", i=4, t=PACK), planes.rearrange("p t (c i) -> p c t i", i=4))
+        def turn_plane(bank, picked, t):
+            pairs = picked[:, t * N:(t + 1) * N].bitcast(F32)
+            for run in range(2):
+                at = (2 * (t % 2) + run) * P
+                nc.tensor.transpose(bank[:, at:at + P], pairs[:, run:HALF:2], identity[:])
 
-        def product(lhs, lhs_fmt, rhs):
-            bank = sums.tile([P, N], F32, name="sum", tag="sum")
-            nc.tensor.matmul_mx(out=bank[:], lhsT=lhs[0].bitcast(lhs_fmt), lhsT_scale=lhs[1],
-                                rhs=rhs[0][:].bitcast(E4M3), rhs_scale=rhs[1][:], start=True, stop=True)
-            return bank
-
-        def gather_and_turn(name, planes, picked, along_slots, h):
-            bank = turns.tile([P, N], F32, name="bank", tag="turn")
-            for t2 in range(2):
-                t = 2 * h + t2
-                gather(picked[:, t * N:(t + 1) * N], planes[t])
-                turn_words(bank, t2, picked[:, t * N:(t + 1) * N])
-            turned = along_slots[:, h * 2 * N:(h + 1) * 2 * N]
-            nc.scalar.copy(turned.bitcast(F32).rearrange("s (p x) -> s p x", x=4),
+        def words_along_slots(name, bank):
+            words = by_scalar(name, 2 * N, BF16)
+            nc.scalar.copy(words[:].bitcast(F32).rearrange("s (p x) -> s p x", x=4),
                            bank[:].rearrange("s (x p) -> s p x", x=4))
-            return turned
+            return words
 
-        def turn_block(name, values):
-            bank = turns.tile([P, N], F32, name="bank", tag="turn")
-            turn_words(bank, 0, values)
-            turned = sb(name + "_turned", N, BF16)
-            nc.scalar.copy(turned[:].bitcast(F32).rearrange("s (r w) -> s r w", w=2),
-                           bank[:, 0:2 * P].rearrange("s (w r) -> s r w", w=2))
-            return turned
+        def planes_by_slot(picked):
+            return picked[:].rearrange("p (t s w e) -> p s w t e", t=PACK, w=2, e=2)
+
+        def turn_dealt(bank, place, values):
+            pairs = values[:].bitcast(F32)
+            for run in range(2):
+                at = (2 * place + run) * P
+                nc.tensor.transpose(bank[:, at:at + P], pairs[:, run * P:(run + 1) * P], identity[:])
+
+        def turned_words(name, bank, count):
+            words = by_scalar(name, count * N, BF16)
+            nc.scalar.copy(words[:].bitcast(F32).rearrange("s (b r w) -> s b r w", b=count, w=2),
+                           bank[:, 0:2 * count * P].rearrange("s (b w r) -> s b r w", b=count, w=2))
+            return words
+
+        def turned_block(name, values):
+            bank = new_bank()
+            turn_dealt(bank, 0, values)
+            return turned_words(name, bank, 1)
 
         def in_feature_order(bank):
             return bank[:].rearrange("r (h p t) -> r p h t", h=2, t=2)
@@ -145,97 +184,166 @@ def tile_attend_ggau_kernel(tc, qT, kT, vT, dy, u, us, ts, tv, offs, out_0, out_
         def as_features(tile):
             return tile[:].rearrange("r (p h t) -> r p h t", h=2, t=2)
 
-        half_cols = [slice(h * (N // 2), (h + 1) * (N // 2)) for h in range(2)]
-
-        k_picked = sb("k_picked", PACK * N, BF16)
-        k_turned = sb("k_turned", PACK * N, BF16)
-        k_turned0 = gather_and_turn("k", k_planes, k_picked, k_turned, 0)
-        ts_picked = sb("ts_picked", N, F32)
-        tv_picked = sb("tv_picked", N, F32)
-        gather(ts_picked[:], ts_window)
-        gather(tv_picked[:], tv_window)
+        ts_row = gathered_scale("ts", ts_window)
+        tv_row = gathered_scale("tv", tv_window)
         us_cols = row_to_columns("us_cols", us_row)
-        ts_cols = row_to_columns("ts_cols", ts_picked)
-        tv_cols = row_to_columns("tv_cols", tv_picked)
+        ts_cols = row_to_columns("ts_cols", ts_row)
+        tv_cols = row_to_columns("tv_cols", tv_row)
         neg_c_cols = keep.tile([P, BLOCKS], F32, name="neg_c_cols")
-        nc.vector.scalar_tensor_tensor(neg_c_cols[:], ts_cols[:], -1.0, tv_cols[:], ALU.mult, ALU.mult)
-        ts_rows = columns_to_rows("ts_rows", ts_cols)
-        tv_rows = columns_to_rows("tv_rows", tv_cols)
-        neg_c_rows = columns_to_rows("neg_c_rows", neg_c_cols)
-        k_turned1 = gather_and_turn("k", k_planes, k_picked, k_turned, 1)
-        k_words = sb("k_words", PACK * N, BF16)
-        interleave(nc.vector.tensor_copy, k_words[:], k_picked[:].rearrange("p (t i) -> p t i", t=PACK))
-        k_features = quantise("k_features", k_words[:], E4M3)
+        nc.gpsimd.tensor_tensor(neg_c_cols[:], ts_cols[:], tv_cols[:], ALU.mult)
+        nc.gpsimd.tensor_scalar(neg_c_cols[:], neg_c_cols[:], -1.0, 0.0, ALU.mult, ALU.add)
+        tv_bank = new_bank()
+        columns_to_rows(tv_bank, tv_cols)
+        tv_rows = kept("tv_rows", N, F32)
+        nc.scalar.activation(tv_rows[:], tv_bank[:], ACT.Copy, scale=1.0)
+        neg_c_rows = held.tile([P, N], F32, name="neg_c_rows")
+        columns_to_rows(neg_c_rows, neg_c_cols)
 
-        q_mx = []
+        k_picked = kept("k_picked", PACK * N, BF16)
+        v_picked = kept("v_picked", PACK * N, BF16)
+        k_banks = []
+        k_words = []
+        for t in range(PACK):
+            gather_plane(k_picked, k_planes, t)
+            if t % 2 == 0:
+                k_banks.append(new_bank())
+            turn_plane(k_banks[t // 2], k_picked, t)
+            if t == 1:
+                k_words.append(words_along_slots("k_turned0", k_banks[0]))
+        k_woven = kept("k_woven", PACK * N, BF16)
+        nc.vector.tensor_copy(k_woven[:].rearrange("p (w s e t) -> p s w t e", w=2, e=2, t=PACK), planes_by_slot(k_picked))
+        q_woven = []
         for h in range(2):
-            q_words = sb("q_words%d" % h, PACK * N // 2, BF16)
-            interleave(nc.scalar.copy, q_words[:], q_halves[h][:])
-            q_mx.append(quantise("q%d" % h, q_words[:], E4M3))
+            q_woven.append(by_scalar("q_woven%d" % h, PACK * HALF, BF16))
+            nc.scalar.copy(q_woven[h][:].rearrange("p (c i t) -> p c t i", i=4, t=PACK),
+                           q_halves[h][:].rearrange("p t (c i) -> p c t i", i=4))
+        q_mx = [quantise("q0", q_woven[0], E4M3)]
+        k_features = quantise("k_features", k_woven, E4M3)
+        q_mx.append(quantise("q1", q_woven[1], E4M3))
+        k_words.append(words_along_slots("k_turned1", k_banks[1]))
 
-        v_picked = sb("v_picked", PACK * N, BF16)
-        v_turned = sb("v_turned", PACK * N, BF16)
+        score_banks = {}
+        for h in range(2):
+            for pair in range(2):
+                score_banks[h, pair] = new_bank()
+                for t in range(2):
+                    mx_pass(score_banks[h, pair][:, t * HALF:(t + 1) * HALF], block_of(k_features, 2 * pair + t), E4M3, q_mx[h])
+        gather_plane(v_picked, v_planes, 0)
+        k_slots = quantise_halves("k_slots", k_words)
+        z_banks = []
+        for h in range(2):
+            scaled = []
+            for pair in range(2):
+                scaled.append(by_scalar("scaled", N, F32))
+                for t in range(2):
+                    cols = slice(t * HALF, (t + 1) * HALF)
+                    nc.scalar.activation(scaled[pair][:, cols], score_banks[h, pair][:, cols], ACT.Copy,
+                                         scale=ts_cols[:, 2 * pair + t:2 * pair + t + 1])
+            for j in range(2):
+                z_banks.append(new_bank())
+                for t in range(BLOCKS):
+                    at = (t % 2) * HALF + j * P
+                    nc.tensor.transpose(z_banks[2 * h + j][:, t * P:(t + 1) * P], scaled[t // 2][:, at:at + P], identity[:])
 
-        def scores(j):
-            codes, scales = q_mx[j // 2]
-            cols = slice((j % 2) * P, (j % 2 + 1) * P)
-            a = product((codes[:, cols], scales[:, cols]), E4M3, k_features)
-            z = sb("z%d" % j, N, F32)
-            nc.vector.tensor_tensor(z[:], a[:], ts_rows[:], ALU.mult)
-            s = sb("s%d" % j, N, F32)
-            nc.scalar.activation(s[:], z[:], ACT.Sigmoid, scale=us_cols[:, j:j + 1])
-            sq = sb("sq%d" % j, N, F32)
-            nc.scalar.activation(sq[:], s[:], ACT.Square, scale=-1.0, bias=half[:])
-            return s, sq
+        s, w, m = [], [], []
 
-        def weights(j, s, sq):
-            w = ring_tile("rounded", BF16)
-            nc.vector.tensor_tensor(w[:], s[:], tv_rows[:], ALU.mult)
-            w_turned = turn_block("w%d" % j, w[:])
-            m = sb("m%d" % j, N, F32)
-            nc.vector.scalar_tensor_tensor(m[:], sq[:], -0.25, neg_c_rows[:], ALU.add, ALU.mult)
-            return w_turned, m
+        def weights(j):
+            s.append(by_scalar("s", N, F32))
+            nc.scalar.activation(s[j][:], z_banks[j][:], ACT.Sigmoid, scale=us_cols[:, j:j + 1])
+            w.append(kept("w%d" % j, N, BF16))
+            nc.gpsimd.tensor_tensor(w[j][:], s[j][:], tv_rows[:], ALU.mult)
 
-        def gate_gradient(j):
-            o = product((w_mx[j][0][:], w_mx[j][1][:]), E4M3, v_slots)
-            result = sb("result0_%d" % j, N, F32)
-            nc.vector.tensor_tensor(as_features(result), in_feature_order(o), as_features(dy_blocks[j]), ALU.mult)
-            nc.sync.dma_start(out_0[j * P:(j + 1) * P, :], result[:])
+        def slopes(j):
+            square = by_scalar("square", N, F32)
+            nc.scalar.activation(square[:], s[j][:], ACT.Square, scale=-1.0, bias=one_half[:])
+            m.append(by_vector("m", N, F32))
+            nc.vector.scalar_tensor_tensor(m[j][:], square[:], -0.25, neg_c_rows[:], ALU.add, ALU.mult)
+
+        gather_plane(v_picked, v_planes, 1)
+        for j in (0, 1):
+            weights(j)
+        for j in (0, 1):
+            slopes(j)
+        for j in (2, 3):
+            weights(j)
+        gather_plane(v_picked, v_planes, 2)
+        for j in (2, 3):
+            slopes(j)
+
+        def turned_value_pair(h):
+            bank = new_bank()
+            for t in (2 * h, 2 * h + 1):
+                turn_plane(bank, v_picked, t)
+            return bank
+
+        v_words = [words_along_slots("v_turned0", turned_value_pair(0))]
+        w_words = []
+        for h in range(2):
+            w_bank = new_bank()
+            for j in range(2):
+                turn_dealt(w_bank, j, w[2 * h + j])
+            w_words.append(turned_words("w_turned", w_bank, 2))
+
+        def weave_values(half):
+            woven = by_scalar("v_woven", 2 * N, BF16)
+            nc.scalar.copy(woven[:].rearrange("p (s e t) -> p s t e", e=2, t=PACK), planes_by_slot(v_picked)[:, :, half])
+            return woven
 
         def output_gradient(j):
-            do = ring_tile("rounded", BF16)
-            nc.vector.tensor_tensor(do[:], dy_blocks[j][:], u_blocks[j][:], ALU.mult)
-            return turn_block("do%d" % j, do[:])
+            do = by_vector("do", N, BF16)
+            nc.vector.tensor_tensor(as_dealt(do[:]), dealt(dy_blocks[j][:]), dealt(u_blocks[j][:]), ALU.mult)
+            return turned_block("do_turned", do)
 
-        def score_gradient(j, do_mx):
-            b = product((do_mx[0][:], do_mx[1][:]), E5M2, v_features)
-            g = ring_tile("rounded", BF16)
-            nc.vector.scalar_tensor_tensor(g[:], b[:], us_cols[:, j:j + 1], wm[j][1][:], ALU.mult, ALU.mult)
-            return turn_block("g%d" % j, g[:])
+        gather_plane(v_picked, v_planes, 3)
+        v_bank = turned_value_pair(1)
+        v_woven = {1: weave_values(1)}
+        do_words = [output_gradient(0)]
+        w_mx = [quantise("w%d" % h, w_words[h], E4M3) for h in range(2)]
+        v_words.append(words_along_slots("v_turned1", v_bank))
+        v_woven[0] = weave_values(0)
+        do_words.append(output_gradient(1))
+        do_mx = [quantise("do0", do_words[0], E5M2)]
+        v_slots = quantise_halves("v_slots", v_words)
 
-        def query_gradient(j, g_mx):
-            dq = product((g_mx[0][:], g_mx[1][:]), E5M2, k_slots)
-            result = sb("result1_%d" % j, N, F32)
-            nc.scalar.copy(as_features(result), in_feature_order(dq))
+        def weighted_values(j):
+            return product(block_of(w_mx[j // 2], j % 2), E4M3, v_slots)
+
+        o_banks = [weighted_values(0)]
+        do_words.append(output_gradient(2))
+        v_features = quantise_halves("v_features", v_woven)
+        b_banks = [product(block_of(do_mx[0], 0), E5M2, v_features)]
+
+        def values_times_gradient(j):
+            do_mx.append(quantise("do%d" % j, do_words[j], E5M2))
+            b_banks.append(product(block_of(do_mx[j], 0), E5M2, v_features))
+
+        values_times_gradient(1)
+        do_words.append(output_gradient(3))
+
+        g_words, dq_banks = [], []
+
+        def query_gradient(j):
+            dq_banks.append(product(block_of(quantise("g%d" % j, g_words[j], E5M2), 0), E5M2, k_slots))
+
+        def store_out_1(j):
+            result = by_scalar("result_1", N, F32)
+            nc.scalar.copy(as_features(result), in_feature_order(dq_banks[j]))
             nc.sync.dma_start(out_1[j * P:(j + 1) * P, :], result[:])
 
-
-        ssq = [scores(j) for j in range(2)]
-        gather_and_turn("v", v_planes, v_picked, v_turned, 0)
-        ssq.extend([scores(j) for j in range(2, 4)])
-        gather_and_turn("v", v_planes, v_picked, v_turned, 1)
-        v_words = sb("v_words", PACK * N, BF16)
-        interleave(nc.scalar.copy, v_words[:], v_picked[:].rearrange("p (t i) -> p t i", t=PACK))
-        v_features = quantise("v_features", v_words[:], E4M3)
-        wm = [weights(j, ssq[j][0], ssq[j][1]) for j in range(BLOCKS)]
-        v_slots = quantise("v_slots", v_turned[:], E4M3)
-        g_turned = []
         for j in range(BLOCKS):
-            do_mx = quantise("do%d" % j, output_gradient(j)[:], E5M2)
-            g_turned.append(score_gradient(j, do_mx))
-        k_slots = quantise("k_slots", k_turned[:], E4M3)
-        for j in range(BLOCKS):
-            query_gradient(j, quantise("g%d" % j, g_turned[j][:], E5M2))
-        w_mx = [quantise("w%d" % j, wm[j][0][:], E4M3) for j in range(BLOCKS)]
-        for j in range(BLOCKS):
-            gate_gradient(j)
+            g = by_vector("g", N, BF16)
+            nc.vector.scalar_tensor_tensor(g[:], b_banks[j][:], us_cols[:, j:j + 1], m[j][:], ALU.mult, ALU.mult)
+            g_words.append(turned_block("g_turned", g))
+            if j + 2 < BLOCKS:
+                values_times_gradient(j + 2)
+            if j >= 1:
+                query_gradient(j - 1)
+            result = by_vector("result_0", N, F32)
+            nc.vector.tensor_tensor(as_features(result), in_feature_order(o_banks[j]), as_features(dy_blocks[j]), ALU.mult)
+            nc.sync.dma_start(out_0[j * P:(j + 1) * P, :], result[:])
+            if j + 1 < BLOCKS:
+                o_banks.append(weighted_values(j + 1))
+            if j >= 1:
+                store_out_1(j - 1)
+        query_gradient(BLOCKS - 1)
+        store_out_1(BLOCKS - 1)

from contextlib import ExitStack

import concourse.mybir as mybir
from concourse.masks import make_identity

F32 = mybir.dt.float32
BF16 = mybir.dt.bfloat16
U32 = mybir.dt.uint32
U16 = mybir.dt.uint16
U8 = mybir.dt.uint8
E4M3 = mybir.dt.float8_e4m3fn_x4
E5M2 = mybir.dt.float8_e5m2_x4
ACT = mybir.ActivationFunctionType
ALU = mybir.AluOpType

P = 128
PACK = 4
N = 512
HALF = N // 2
TOKENS = 2048
BLOCKS = N // P
LAST = P - 1

VECTOR_TILES = 33
SCALAR_TILES = 18
PASSING_BANKS = 7

FLOPS = 4 * 2 * N * N * N
BYTES = 4 * (2 * N * TOKENS + 5 * N * N + N + 2 * TOKENS) + 2 * P * (N // 16)


def tile_attend_ggau_kernel(tc, qT, kT, vT, dy, u, us, ts, tv, offs, out_0, out_1):
    nc = tc.nc
    with ExitStack() as ctx:
        keep = ctx.enter_context(tc.tile_pool(name="keep", bufs=1))
        scalar_ring = ctx.enter_context(tc.tile_pool(name="scalar_ring", bufs=SCALAR_TILES))
        vector_ring = ctx.enter_context(tc.tile_pool(name="vector_ring", bufs=VECTOR_TILES))
        banks = ctx.enter_context(tc.psum_pool(name="banks", bufs=PASSING_BANKS))
        held = ctx.enter_context(tc.psum_pool(name="held", bufs=1))

        def kept(name, cols, dtype):
            return keep.tile([P, cols], dtype, name=name, align_bytes=64)

        def by_scalar(name, cols, dtype):
            return scalar_ring.tile([P, cols], dtype, name=name, tag="by_scalar", align_bytes=64)

        def by_vector(name, cols, dtype):
            return vector_ring.tile([P, cols], dtype, name=name, tag="by_vector", align_bytes=64)

        def new_bank():
            return banks.tile([P, N], F32, name="bank", tag="bank")

        offsets = keep.tile([P, N // 16], U16, name="offsets")
        nc.sync.dma_start(offsets[:], offs)

        ts_window = kept("ts_window", TOKENS, F32)
        tv_window = kept("tv_window", TOKENS, F32)
        us_row = kept("us_row", N, F32)
        nc.sync.dma_start(ts_window[LAST:P, :], ts[0:1, :])
        nc.sync.dma_start(tv_window[LAST:P, :], tv[0:1, :])
        nc.sync.dma_start(us_row[LAST:P, :], us.rearrange("r o -> o r"))

        k_planes = [kept("k_plane%d" % t, TOKENS, F32) for t in range(PACK)]
        v_planes = [kept("v_plane%d" % t, TOKENS, F32) for t in range(PACK)]
        q_halves = [keep.tile([P, PACK, HALF], F32, name="q_half%d" % h) for h in range(2)]
        dy_blocks = [kept("dy%d" % j, N, F32) for j in range(BLOCKS)]
        u_blocks = [kept("u%d" % j, N, F32) for j in range(BLOCKS)]
        for t in range(PACK):
            nc.sync.dma_start(k_planes[t][:], kT.rearrange("(p t) w -> t p w", t=PACK)[t])

        zero = keep.tile([P, 1], F32, name="zero")
        one_half = keep.tile([P, 1], F32, name="one_half")
        nc.vector.memset(zero[:], 0.0)
        nc.scalar.activation(one_half[:], zero[:], ACT.Sigmoid)

        identity = kept("identity", P, F32)
        make_identity(nc, identity[:])
        nc.vector.memset(ts_window[0:LAST, :], 0.0)
        nc.gpsimd.memset(tv_window[0:LAST, :], 0.0)
        nc.vector.memset(us_row[0:LAST, :], 0.0)

        for h in range(2):
            nc.sync.dma_start(q_halves[h][:], qT.rearrange("(p t) r -> p t r", t=PACK)[:, :, h * HALF:(h + 1) * HALF])
        for t in range(PACK):
            nc.sync.dma_start(v_planes[t][:], vT.rearrange("(p t) w -> t p w", t=PACK)[t])
        for j in range(BLOCKS):
            nc.sync.dma_start(dy_blocks[j][:], dy[j * P:(j + 1) * P, :])
            nc.sync.dma_start(u_blocks[j][:], u[j * P:(j + 1) * P, :])

        def gather(out, window):
            nc.vector.tensor_copy(out, window[:].indirect(offsets[:]))

        def quantise(name, values, fmt):
            words = values.shape[1] // PACK
            codes = by_vector(name + "_codes", words, U32)
            scales = kept(name + "_scales", words, U8)
            nc.vector.quantize_mx(out=codes[:].bitcast(fmt), scales=scales[:], in_=values[:])
            return codes, scales

        def quantise_halves(name, halves):
            codes = by_vector(name + "_codes", N, U32)
            scales = kept(name + "_scales", N, U8)
            for h in (1, 0):
                cols = slice(h * HALF, (h + 1) * HALF)
                nc.vector.quantize_mx(out=codes[:, cols].bitcast(E4M3), scales=scales[:, cols], in_=halves[h][:])
            return codes, scales

        def block_of(operand, j):
            cols = slice(j * P, (j + 1) * P)
            return operand[0][:, cols], operand[1][:, cols]

        def mx_pass(out, stationary, stationary_fmt, moving):
            nc.tensor.matmul_mx(out=out, lhsT=stationary[0].bitcast(stationary_fmt), lhsT_scale=stationary[1],
                                rhs=moving[0][:].bitcast(E4M3), rhs_scale=moving[1][:], start=True, stop=True)

        def product(stationary, stationary_fmt, moving):
            bank = new_bank()
            mx_pass(bank[:], stationary, stationary_fmt, moving)
            return bank

        def dealt(row):
            return row.rearrange("p (s w e) -> p w s e", w=2, e=2)

        def as_dealt(row):
            return row.rearrange("p (w s e) -> p w s e", w=2, e=2)

        def gathered_scale(name, window):
            picked = kept(name + "_picked", N, F32)
            gather(picked[:], window)
            row = by_scalar(name + "_dealt", N, F32)
            nc.scalar.copy(as_dealt(row[:]), dealt(picked[:]))
            return row

        def row_to_columns(name, row):
            bank = new_bank()
            for j in range(BLOCKS):
                nc.tensor.transpose(bank[:, j * P:(j + 1) * P], row[:, j * P:(j + 1) * P], identity[:])
            columns = keep.tile([P, BLOCKS], F32, name=name)
            nc.scalar.copy(columns[:], bank[:, LAST:N:P])
            return columns

        def columns_to_rows(bank, columns):
            for j in range(BLOCKS):
                nc.tensor.transpose(bank[:, j * P:(j + 1) * P], columns[:, j:j + 1].to_broadcast([P, P]), identity[:])

        def gather_plane(picked, planes, t):
            gather(picked[:, t * N:(t + 1) * N], planes[t])

        def turn_plane(bank, picked, t):
            pairs = picked[:, t * N:(t + 1) * N].bitcast(F32)
            for run in range(2):
                at = (2 * (t % 2) + run) * P
                nc.tensor.transpose(bank[:, at:at + P], pairs[:, run:HALF:2], identity[:])

        def words_along_slots(name, bank):
            words = by_scalar(name, 2 * N, BF16)
            nc.scalar.copy(words[:].bitcast(F32).rearrange("s (p x) -> s p x", x=4),
                           bank[:].rearrange("s (x p) -> s p x", x=4))
            return words

        def planes_by_slot(picked):
            return picked[:].rearrange("p (t s w e) -> p s w t e", t=PACK, w=2, e=2)

        def turn_dealt(bank, place, values):
            pairs = values[:].bitcast(F32)
            for run in range(2):
                at = (2 * place + run) * P
                nc.tensor.transpose(bank[:, at:at + P], pairs[:, run * P:(run + 1) * P], identity[:])

        def turned_words(name, bank, count):
            words = by_scalar(name, count * N, BF16)
            nc.scalar.copy(words[:].bitcast(F32).rearrange("s (b r w) -> s b r w", b=count, w=2),
                           bank[:, 0:2 * count * P].rearrange("s (b w r) -> s b r w", b=count, w=2))
            return words

        def turned_block(name, values):
            bank = new_bank()
            turn_dealt(bank, 0, values)
            return turned_words(name, bank, 1)

        def in_feature_order(bank):
            return bank[:].rearrange("r (h p t) -> r p h t", h=2, t=2)

        def as_features(tile):
            return tile[:].rearrange("r (p h t) -> r p h t", h=2, t=2)

        ts_row = gathered_scale("ts", ts_window)
        tv_row = gathered_scale("tv", tv_window)
        us_cols = row_to_columns("us_cols", us_row)
        ts_cols = row_to_columns("ts_cols", ts_row)
        tv_cols = row_to_columns("tv_cols", tv_row)
        neg_c_cols = keep.tile([P, BLOCKS], F32, name="neg_c_cols")
        nc.gpsimd.tensor_tensor(neg_c_cols[:], ts_cols[:], tv_cols[:], ALU.mult)
        nc.gpsimd.tensor_scalar(neg_c_cols[:], neg_c_cols[:], -1.0, 0.0, ALU.mult, ALU.add)
        tv_bank = new_bank()
        columns_to_rows(tv_bank, tv_cols)
        tv_rows = kept("tv_rows", N, F32)
        nc.scalar.activation(tv_rows[:], tv_bank[:], ACT.Copy, scale=1.0)
        neg_c_rows = held.tile([P, N], F32, name="neg_c_rows")
        columns_to_rows(neg_c_rows, neg_c_cols)

        k_picked = kept("k_picked", PACK * N, BF16)
        v_picked = kept("v_picked", PACK * N, BF16)
        k_banks = []
        k_words = []
        for t in range(PACK):
            gather_plane(k_picked, k_planes, t)
            if t % 2 == 0:
                k_banks.append(new_bank())
            turn_plane(k_banks[t // 2], k_picked, t)
            if t == 1:
                k_words.append(words_along_slots("k_turned0", k_banks[0]))
        k_woven = kept("k_woven", PACK * N, BF16)
        nc.vector.tensor_copy(k_woven[:].rearrange("p (w s e t) -> p s w t e", w=2, e=2, t=PACK), planes_by_slot(k_picked))
        q_woven = []
        for h in range(2):
            q_woven.append(by_scalar("q_woven%d" % h, PACK * HALF, BF16))
            nc.scalar.copy(q_woven[h][:].rearrange("p (c i t) -> p c t i", i=4, t=PACK),
                           q_halves[h][:].rearrange("p t (c i) -> p c t i", i=4))
        q_mx = [quantise("q0", q_woven[0], E4M3)]
        k_features = quantise("k_features", k_woven, E4M3)
        q_mx.append(quantise("q1", q_woven[1], E4M3))
        k_words.append(words_along_slots("k_turned1", k_banks[1]))

        score_banks = {}
        for h in range(2):
            for pair in range(2):
                score_banks[h, pair] = new_bank()
                for t in range(2):
                    mx_pass(score_banks[h, pair][:, t * HALF:(t + 1) * HALF], block_of(k_features, 2 * pair + t), E4M3, q_mx[h])
        gather_plane(v_picked, v_planes, 0)
        k_slots = quantise_halves("k_slots", k_words)
        z_banks = []
        for h in range(2):
            scaled = []
            for pair in range(2):
                scaled.append(by_scalar("scaled", N, F32))
                for t in range(2):
                    cols = slice(t * HALF, (t + 1) * HALF)
                    nc.scalar.activation(scaled[pair][:, cols], score_banks[h, pair][:, cols], ACT.Copy,
                                         scale=ts_cols[:, 2 * pair + t:2 * pair + t + 1])
            for j in range(2):
                z_banks.append(new_bank())
                for t in range(BLOCKS):
                    at = (t % 2) * HALF + j * P
                    nc.tensor.transpose(z_banks[2 * h + j][:, t * P:(t + 1) * P], scaled[t // 2][:, at:at + P], identity[:])

        s, w, m = [], [], []

        def weights(j):
            s.append(by_scalar("s", N, F32))
            nc.scalar.activation(s[j][:], z_banks[j][:], ACT.Sigmoid, scale=us_cols[:, j:j + 1])
            w.append(kept("w%d" % j, N, BF16))
            nc.gpsimd.tensor_tensor(w[j][:], s[j][:], tv_rows[:], ALU.mult)

        def slopes(j):
            square = by_scalar("square", N, F32)
            nc.scalar.activation(square[:], s[j][:], ACT.Square, scale=-1.0, bias=one_half[:])
            m.append(by_vector("m", N, F32))
            nc.vector.scalar_tensor_tensor(m[j][:], square[:], -0.25, neg_c_rows[:], ALU.add, ALU.mult)

        gather_plane(v_picked, v_planes, 1)
        for j in (0, 1):
            weights(j)
        for j in (0, 1):
            slopes(j)
        for j in (2, 3):
            weights(j)
        gather_plane(v_picked, v_planes, 2)
        for j in (2, 3):
            slopes(j)

        def turned_value_pair(h):
            bank = new_bank()
            for t in (2 * h, 2 * h + 1):
                turn_plane(bank, v_picked, t)
            return bank

        v_words = [words_along_slots("v_turned0", turned_value_pair(0))]
        w_words = []
        for h in range(2):
            w_bank = new_bank()
            for j in range(2):
                turn_dealt(w_bank, j, w[2 * h + j])
            w_words.append(turned_words("w_turned", w_bank, 2))

        def weave_values(half):
            woven = by_scalar("v_woven", 2 * N, BF16)
            nc.scalar.copy(woven[:].rearrange("p (s e t) -> p s t e", e=2, t=PACK), planes_by_slot(v_picked)[:, :, half])
            return woven

        def output_gradient(j):
            do = by_vector("do", N, BF16)
            nc.vector.tensor_tensor(as_dealt(do[:]), dealt(dy_blocks[j][:]), dealt(u_blocks[j][:]), ALU.mult)
            return turned_block("do_turned", do)

        gather_plane(v_picked, v_planes, 3)
        v_bank = turned_value_pair(1)
        v_woven = {1: weave_values(1)}
        do_words = [output_gradient(0)]
        w_mx = [quantise("w%d" % h, w_words[h], E4M3) for h in range(2)]
        v_words.append(words_along_slots("v_turned1", v_bank))
        v_woven[0] = weave_values(0)
        do_words.append(output_gradient(1))
        do_mx = [quantise("do0", do_words[0], E5M2)]
        v_slots = quantise_halves("v_slots", v_words)

        def weighted_values(j):
            return product(block_of(w_mx[j // 2], j % 2), E4M3, v_slots)

        o_banks = [weighted_values(0)]
        do_words.append(output_gradient(2))
        v_features = quantise_halves("v_features", v_woven)
        b_banks = [product(block_of(do_mx[0], 0), E5M2, v_features)]

        def values_times_gradient(j):
            do_mx.append(quantise("do%d" % j, do_words[j], E5M2))
            b_banks.append(product(block_of(do_mx[j], 0), E5M2, v_features))

        values_times_gradient(1)
        do_words.append(output_gradient(3))

        g_words, dq_banks = [], []

        def query_gradient(j):
            dq_banks.append(product(block_of(quantise("g%d" % j, g_words[j], E5M2), 0), E5M2, k_slots))

        def store_out_1(j):
            result = by_scalar("result_1", N, F32)
            nc.scalar.copy(as_features(result), in_feature_order(dq_banks[j]))
            nc.sync.dma_start(out_1[j * P:(j + 1) * P, :], result[:])

        for j in range(BLOCKS):
            g = by_vector("g", N, BF16)
            nc.vector.scalar_tensor_tensor(g[:], b_banks[j][:], us_cols[:, j:j + 1], m[j][:], ALU.mult, ALU.mult)
            g_words.append(turned_block("g_turned", g))
            if j + 2 < BLOCKS:
                values_times_gradient(j + 2)
            if j >= 1:
                query_gradient(j - 1)
            result = by_vector("result_0", N, F32)
            nc.vector.tensor_tensor(as_features(result), in_feature_order(o_banks[j]), as_features(dy_blocks[j]), ALU.mult)
            nc.sync.dma_start(out_0[j * P:(j + 1) * P, :], result[:])
            if j + 1 < BLOCKS:
                o_banks.append(weighted_values(j + 1))
            if j >= 1:
                store_out_1(j - 1)
        query_gradient(BLOCKS - 1)
        store_out_1(BLOCKS - 1)
